import numpy as np
import ml_dtypes


def mxq(x, axis, fmt="e4m3"):
    dtype, down = {"e4m3": (ml_dtypes.float8_e4m3fn, 7), "e5m2": (ml_dtypes.float8_e5m2, 14)}[fmt]
    v = np.moveaxis(np.asarray(x, np.float32).astype(ml_dtypes.bfloat16).astype(np.float64), axis, -1)
    blocks = v.reshape(v.shape[:-1] + (-1, 32))
    amax = np.abs(blocks).max(-1, keepdims=True)
    byte = np.maximum(np.where(amax > 0, np.frexp(amax)[1] - 1 + 127, 0) - down, 1)
    scale = np.exp2(byte - 127.0)
    codes = (blocks / scale).astype(np.float32).astype(dtype).astype(np.float64)
    return np.moveaxis((codes * scale).reshape(v.shape), -1, axis)


WIDE = False


def mx_kscale(k):
    if not WIDE:
        return np.ones(k)
    levels = np.array([18, -18])
    if k % 512:
        return np.exp2(np.random.permutation(np.resize(levels, k // 32))).repeat(32)
    a = np.empty((k // 512, 16))
    for p in range(k // 512):
        a[p, :8] = np.random.permutation(np.resize(levels, 8))
        for g in range(8):
            far = levels[np.abs(levels - a[p, g]) >= 10]
            a[p, g + 8] = far[np.random.randint(len(far))]
    return np.exp2(a.ravel()).repeat(32)


def f64(x):
    return np.asarray(x).astype(np.float64)


def striped(idx):
    return np.tile(np.asarray(idx).reshape(-1, 16).T, (8, 1)).astype(np.uint16)


def unstriped(offs):
    return offs[:16].T.reshape(-1).astype(np.int64)


B, N, T, D, DV = 2, 512, 2048, 512, 1024


def setup_inputs():
    n = np.random.standard_normal
    idx = np.random.permutation(T)[:B * N]
    u = np.ones(T)
    u[idx] = mx_kscale(B * N)
    coarse = lambda x: x.astype(np.float32).astype(ml_dtypes.bfloat16).astype(np.float64)
    r = np.random.randint(8, 33, T) / 16.0 * u
    return {
        "xT": (n((D, T)) / np.sqrt(N) / u).astype(np.float32),
        "dyT": (coarse(n((DV, T)))).astype(np.float32),
        "hT": coarse(n((DV, T))).astype(np.float32),
        "ts": np.tile(r, (128, 1)).astype(np.float32),
        "offs": striped(idx),
    }


def reference(xT, dyT, hT, ts, offs):
    idx = unstriped(offs)
    pick = lambda x: x[:, idx].reshape(x.shape[0], B, N).transpose(1, 0, 2)
    h = pick(f64(hT))
    dz = pick(f64(ts))[:, :1, :] * pick(f64(dyT)) * 2.0 * np.maximum(h, 0.0)
    gw = mxq(pick(f64(xT)), 2, "e4m3") @ mxq(dz, 2, "e5m2").transpose(0, 2, 1)
    return gw

@@ -1,0 +1,297 @@
+from contextlib import ExitStack
+
+import concourse.mybir as mybir
+from concourse.masks import make_identity
+
+B, N, T, D, DV = 2, 512, 2048, 512, 1024
+FLOPS = 2 * B * N * D * DV
+BYTES = 4 * (D * T + 2 * DV * T + T + B * D * DV) + 2 * 128 * B * N // 16
+
+F32 = mybir.dt.float32
+BF16 = mybir.dt.bfloat16
+U32 = mybir.dt.uint32
+U16 = mybir.dt.uint16
+U8 = mybir.dt.uint8
+E4M3 = mybir.dt.float8_e4m3fn_x4
+E5M2 = mybir.dt.float8_e5m2_x4
+MULT = mybir.AluOpType.mult
+MAX = mybir.AluOpType.max
+COPY = mybir.ActivationFunctionType.Copy
+RELU = mybir.ActivationFunctionType.Relu
+
+P = 128
+BANK = 512
+LIST_COLS = N // 16
+D_BLOCKS = D // P
+N_BLOCKS = DV // P
+LOADS = "h0 h1 y0 h2 y1 h3 x0 y2 h4 y3 y4 h5 x1 y5 h6 y6 x2 h7 y7 x3".split()
+ON_GPSIMD = (0, 1, 2, 4, 5, 6)
+H_SLOT = {0: "first0", 1: "first1", 2: "ts_cols0", 3: "y0", 4: "y1", 5: "y2", 6: "y0", 7: "y1"}
+DY_SLOT = {(0, 0): "h0", (1, 0): "h1", (2, 0): "h2", (3, 0): "h0", (4, 0): "h1", (5, 0): "h2", (6, 0): "h0", (7, 0): "h1", (7, 1): "d71"}
+RELU_SLOT = {0: "ts_cols1", 1: "first0"}
+DZ_SLOT = {0: "ts_listed", 1: "ts_window", 2: "dz", 3: "ts_listed", 4: "ts_window", 5: "dz", 6: "ts_listed"}
+TURNED_SLOT = "x2"
+DZ_BANK = "BCABBAACA"
+X_BANK = "BBCCA"
+CODE_WORDS = {'h5': 256, 'h6': 1024, 'h4': 256, 'y7': 256, 'c1': 1024, 'c3': 256}
+STAGE_BANKS = {'first0': 2, 'first1': 2, 'ts_cols0': 2, 'ts_cols1': 2, 'h3': 4, 'y3': 4}
+
+
+def tile_attend_gex_w_kernel(tc, xT, dyT, hT, ts, offs, out):
+    nc = tc.nc
+    with ExitStack() as ctx:
+        keep = ctx.enter_context(tc.tile_pool(name="keep", bufs=1))
+        slots = ctx.enter_context(tc.tile_pool(name="slots", bufs=1))
+        xwork = ctx.enter_context(tc.tile_pool(name="xwork", bufs=2))
+        turn_psum = ctx.enter_context(tc.psum_pool(name="turn_psum", bufs=1))
+        acc_psum = ctx.enter_context(tc.psum_pool(name="acc_psum", bufs=5))
+
+        def tenant(slot, shape, dtype):
+            return slots.tile(shape, dtype, name="tenant", tag=slot, align_bytes=64)
+
+        offsets = keep.tile([P, B * LIST_COLS], U16, name="offsets")
+        nc.sync.dma_start(offsets[:], offs)
+
+        ts_window = tenant("ts_window", [P, T], F32)
+        nc.sync.dma_start(ts_window[P - 1 : P, :], ts[0:1, :])
+        nc.vector.memset(ts_window[0 : P - 1, :], 0.0)
+
+        sources = {"h": hT, "y": dyT, "x": xT}
+        window = {}
+        for key in LOADS:
+            j = int(key[1])
+            window[key] = tenant(key, [P, T], F32)
+            nc.sync.dma_start(window[key][:], sources[key[0]][j * P : (j + 1) * P, :])
+
+        ident = keep.tile([P, P], F32, name="ident")
+        make_identity(nc, ident[:])
+
+        ts_listed = tenant("ts_listed", [P, B * N], F32)
+        nc.vector.tensor_copy(ts_listed[:], ts_window[:].indirect(offsets[:]))
+        ts_cols = [tenant("ts_cols%d" % g, [P, 4], F32) for g in range(B)]
+        ts2 = keep.tile([P, B * N], F32, name="ts2")
+        for g in range(B):
+            bank = acc_psum.tile([P, 4, P], F32, name="acc", tag="acc")
+            for c in range(4):
+                s0 = g * N + c * P
+                nc.tensor.transpose(bank[:, c, :], ts_listed[:, s0 : s0 + P], ident[:])
+            nc.scalar.copy(ts_cols[g][:], bank[:, :, P - 1])
+        for g in range(B):
+            bank = acc_psum.tile([P, 4, P], F32, name="acc", tag="acc")
+            for c in range(4):
+                nc.tensor.transpose(bank[:, c, :], ts_cols[g][:, c : c + 1].to_broadcast([P, P]), ident[:])
+            nc.scalar.activation(ts2[:, g * N : (g + 1) * N], bank[:].rearrange("p c s -> p (c s)"), COPY, scale=2.0)
+
+        dz_turned = {0: keep.tile([P, B, 4 * BANK], BF16, name="dz_turned", align_bytes=64)}
+        dz_scales = keep.tile([P, B, DV], U8, name="dz_scales", align_bytes=64)
+        x_scales = keep.tile([P, D_BLOCKS, B * P], U8, name="x_scales", align_bytes=64)
+
+        h_listed, dy_listed, x_turned, x_codes, dz_codes, banks = {}, {}, {}, {}, {}, {}
+
+        def list_of(b0, nb):
+            return offsets[:, b0 * LIST_COLS : (b0 + nb) * LIST_COLS]
+
+        def copy_on(engine, dst, src):
+            if engine == "scalar":
+                nc.scalar.copy(dst, src)
+            else:
+                nc.vector.tensor_copy(dst, src)
+
+        def gather_h(j):
+            listed = tenant(H_SLOT[j], [P, B * N], F32)
+            nc.vector.tensor_copy(listed[:], window["h%d" % j][:].indirect(offsets[:]))
+            h_listed[j] = tenant(RELU_SLOT[j], [P, B * N], F32) if j in RELU_SLOT and j in ON_GPSIMD else listed
+            if j in ON_GPSIMD:
+                nc.scalar.activation(h_listed[j][:], listed[:], RELU)
+
+        def gather_dy(j, b0, nb):
+            dy_listed[j, b0] = tenant(DY_SLOT[j, b0], [P, nb * N], F32)
+            nc.vector.tensor_tensor(
+                dy_listed[j, b0][:], window["y%d" % j][:].indirect(list_of(b0, nb)), ts2[:, b0 * N : (b0 + nb) * N], MULT
+            )
+
+        def form_dz(j, b0, nb):
+            dz = tenant(DZ_SLOT.get(j, "dz%d_%d" % (j, b0)), [P, nb * N], BF16)
+            h = h_listed[j][:, b0 * N : (b0 + nb) * N]
+            dy = dy_listed[j, b0][:]
+            if j in ON_GPSIMD:
+                nc.gpsimd.tensor_tensor(dz[:], h, dy, MULT)
+            else:
+                nc.vector.scalar_tensor_tensor(dz[:], h, 0.0, dy, MAX, MULT)
+            pairs = dz[:].bitcast(F32)
+            banks[j, b0] = turn_psum.tile([P, nb, 2, P], F32, name="turn", tag=DZ_BANK[j + b0])
+            for b in range(nb):
+                for u in range(2):
+                    nc.tensor.transpose(banks[j, b0][:, b, u, :], pairs[:, 256 * b + u : 256 * (b + 1) : 2], ident[:])
+
+        def land_dz(j, b0, nb, engine):
+            if j == 4:
+                dz_turned[1] = tenant(TURNED_SLOT, [P, B, 4 * BANK], BF16)
+            dst = dz_turned[j // 4][:].bitcast(F32)[:, b0 : b0 + nb, 2 * P * (j % 4) : 2 * P * (j % 4 + 1)]
+            copy_on(engine, dst.rearrange("p b (r u) -> p b r u", u=2), banks[j, b0][:].rearrange("p b u r -> p b r u"))
+
+        carved = {}
+
+        def carve(slot, words):
+            if slot not in carved:
+                carved[slot] = [tenant(slot, [P, CODE_WORDS[slot]], U32), 0]
+            start = carved[slot][1]
+            carved[slot][1] = start + words
+            return carved[slot][0][:, start : start + words]
+
+        staged = {}
+
+        def stage(slot, banks_wanted):
+            if slot not in staged:
+                staged[slot] = [tenant(slot, [P, STAGE_BANKS[slot], BANK], F32), 0]
+            start = staged[slot][1]
+            staged[slot][1] = start + banks_wanted
+            return staged[slot][0][:, start : start + banks_wanted, :]
+
+        def codes_for_dz(half, tag):
+            dz_codes[half] = carve(tag, B * BANK)
+
+        def quantize_dz(b, j0, j1):
+            half = j0 // 4
+            nc.vector.quantize_mx(
+                dz_codes[half][:, b * BANK + (j0 - 4 * half) * P : b * BANK + (j1 - 4 * half) * P].bitcast(E5M2),
+                dz_scales[:, b, j0 * P : j1 * P],
+                dz_turned[half][:, b, 4 * (j0 - 4 * half) * P : 4 * (j1 - 4 * half) * P],
+            )
+
+        def paired(listed):
+            return listed.rearrange("p (u s e) -> p s u e", u=2, e=2)
+
+        def turn_x(i, b0, nb, listed, engine):
+            pairs = listed.bitcast(F32)
+            bank = turn_psum.tile([P, nb, 2, P], F32, name="turn", tag=X_BANK[i + b0])
+            for b in range(nb):
+                for u in range(2):
+                    w0 = (u * nb + b) * P
+                    nc.tensor.transpose(bank[:, b, u, :], pairs[:, w0 : w0 + P], ident[:])
+            x_turned[i, b0] = tenant("x_turned%d" % i, [P, nb * 4 * P], BF16)
+            dst = x_turned[i, b0][:].bitcast(F32).rearrange("p (b r u) -> p b r u", b=nb, u=2)
+            copy_on(engine, dst, bank[:].rearrange("p b u r -> p b r u"))
+
+        def x_by_scalar(i, tag, engine):
+            x_bf16 = tenant(tag, [P, T], BF16)
+            nc.scalar.activation(x_bf16[:], window["x%d" % i][:], COPY)
+            listed = xwork.tile([P, B * N], BF16, name="x_listed", tag="x_listed")
+            nc.scalar.activation(paired(listed[:]), x_bf16[:].indirect(offsets[:]), COPY)
+            turn_x(i, 0, B, listed[:], engine)
+
+        def gather_x(i, b):
+            nc.vector.tensor_copy(paired(last_listed[:, b, :]), window["x%d" % i][:].indirect(list_of(b, 1)))
+
+        def codes_for_x(i, tag):
+            x_codes[i] = carve(tag, B * P)
+
+        def quantize_x(i, b0, nb):
+            cols = slice(b0 * P, (b0 + nb) * P)
+            nc.vector.quantize_mx(x_codes[i][:, cols].bitcast(E4M3), x_scales[:, i, cols], x_turned[i, b0][:])
+
+        def multiply(half, b, i, engine, dst):
+            acc = acc_psum.tile([P, BANK], F32, name="acc", tag="acc")
+            d_cols = slice(b * P, (b + 1) * P)
+            nc.tensor.matmul_mx(
+                acc[:],
+                lhsT=x_codes[i][:, d_cols].bitcast(E4M3),
+                lhsT_scale=x_scales[:, i, d_cols],
+                rhs=dz_codes[half][:, b * BANK : (b + 1) * BANK].bitcast(E5M2),
+                rhs_scale=dz_scales[:, b, half * BANK : (half + 1) * BANK],
+                start=True,
+                stop=True,
+            )
+            copy_on(engine, dst, acc[:])
+
+        def halves(half, b, i0, i1, slot, engines):
+            result = stage(slot, i1 - i0)
+            for i in range(i0, i1):
+                multiply(half, b, i, engines[i - i0], result[:, i - i0, :])
+            dst = out[b, i0 * P : i1 * P, half * BANK : (half + 1) * BANK]
+            nc.sync.dma_start(dst.rearrange("(i p) n -> p i n", p=P), result)
+
+        def first_half(i, slot, engines):
+            result = stage(slot, B)
+            for b in range(B):
+                multiply(0, b, i, engines[b], result[:, b, :])
+            nc.sync.dma_start(out[:, i * P : (i + 1) * P, 0:BANK].rearrange("b p n -> p b n"), result)
+
+        def last_block(b, i, slot, engines):
+            result = stage(slot, 2)
+            for half in range(2):
+                multiply(half, b, i, engines[half], result[:, half, :])
+            nc.sync.dma_start(out[b, i * P : (i + 1) * P, :], result.rearrange("p h n -> p (h n)"))
+
+        last_listed = None
+        gather_h(0)
+        gather_h(1)
+        gather_dy(0, 0, B)
+        form_dz(0, 0, B)
+        land_dz(0, 0, B, "scalar")
+        gather_h(2)
+        gather_dy(1, 0, B)
+        form_dz(1, 0, B)
+        land_dz(1, 0, B, "scalar")
+        gather_h(3)
+        x_by_scalar(0, "xb", "scalar")
+        gather_dy(2, 0, B)
+        form_dz(2, 0, B)
+        land_dz(2, 0, B, "scalar")
+        gather_h(4)
+        gather_dy(3, 0, B)
+        form_dz(3, 0, B)
+        land_dz(3, 0, B, "scalar")
+        gather_dy(4, 0, B)
+        form_dz(4, 0, B)
+        land_dz(4, 0, B, "scalar")
+        gather_h(5)
+        x_by_scalar(1, "xb", "vector")
+        codes_for_x(1, "h5")
+        quantize_x(1, 0, B)
+        gather_dy(5, 0, B)
+        form_dz(5, 0, B)
+        land_dz(5, 0, B, "scalar")
+        gather_h(6)
+        codes_for_dz(0, "h6")
+        quantize_dz(0, 0, 4)
+        quantize_dz(1, 0, 4)
+        first_half(1, "first0", ["scalar", "scalar"])
+        gather_dy(6, 0, B)
+        form_dz(6, 0, B)
+        land_dz(6, 0, B, "scalar")
+        x_by_scalar(2, "xb", "scalar")
+        codes_for_x(2, "h4")
+        quantize_x(2, 0, B)
+        halves(0, 0, 2, 3, "first1", ["scalar"])
+        halves(0, 1, 2, 3, "first1", ["scalar"])
+        gather_h(7)
+        gather_dy(7, 0, 1)
+        form_dz(7, 0, 1)
+        gather_dy(7, 1, 1)
+        land_dz(7, 0, 1, "vector")
+        form_dz(7, 1, 1)
+        codes_for_x(0, "y7")
+        quantize_x(0, 0, B)
+        halves(0, 0, 0, 1, "ts_cols0", ["scalar"])
+        halves(0, 1, 0, 1, "ts_cols0", ["scalar"])
+        codes_for_dz(1, "c1")
+        quantize_dz(0, 4, 8)
+        land_dz(7, 1, 1, "vector")
+        quantize_dz(1, 4, 8)
+        halves(1, 0, 0, 1, "ts_cols1", ["scalar"])
+        halves(1, 0, 1, 2, "ts_cols1", ["scalar"])
+        halves(1, 0, 2, 3, "h3", ["scalar"])
+        halves(1, 1, 0, 1, "h3", ["scalar"])
+        halves(1, 1, 1, 2, "h3", ["scalar"])
+        halves(1, 1, 2, 3, "h3", ["scalar"])
+        last_listed = tenant("xl", [P, B, N], BF16)
+        gather_x(3, 0)
+        gather_x(3, 1)
+        codes_for_x(3, "c3")
+        turn_x(3, 0, 1, last_listed[:, 0, :], "vector")
+        quantize_x(3, 0, 1)
+        turn_x(3, 1, 1, last_listed[:, 1, :], "vector")
+        quantize_x(3, 1, 1)
+        last_block(0, 3, "y3", ["scalar", "vector"])
+        last_block(1, 3, "y3", ["scalar", "vector"])

@@ -24,17 +24,11 @@ BANK = 512
 LIST_COLS = N // 16
 D_BLOCKS = D // P
 N_BLOCKS = DV // P
-LOADS = "h0 h1 y0 h2 y1 h3 x0 y2 h4 y3 y4 h5 x1 y5 h6 y6 x2 h7 y7 x3".split()
-ON_GPSIMD = (0, 1, 2, 4, 5, 6)
-H_SLOT = {0: "first0", 1: "first1", 2: "ts_cols0", 3: "y0", 4: "y1", 5: "y2", 6: "y0", 7: "y1"}
-DY_SLOT = {(0, 0): "h0", (1, 0): "h1", (2, 0): "h2", (3, 0): "h0", (4, 0): "h1", (5, 0): "h2", (6, 0): "h0", (7, 0): "h1", (7, 1): "d71"}
-RELU_SLOT = {0: "ts_cols1", 1: "first0"}
-DZ_SLOT = {0: "ts_listed", 1: "ts_window", 2: "dz", 3: "ts_listed", 4: "ts_window", 5: "dz", 6: "ts_listed"}
-TURNED_SLOT = "x2"
-DZ_BANK = "BCABBAACA"
-X_BANK = "BBCCA"
-CODE_WORDS = {'h5': 256, 'h6': 1024, 'h4': 256, 'y7': 256, 'c1': 1024, 'c3': 256}
-STAGE_BANKS = {'first0': 2, 'first1': 2, 'ts_cols0': 2, 'ts_cols1': 2, 'h3': 4, 'y3': 4}
+WINDOW_BYTES = 4 * T
+X_LANDS = {"h1": 0, "h5": 1, "h7": 2}
+ROOMS = {4: "h0"}
+HALF = WINDOW_BYTES // 2
+LOADS = "h0 y0 y1 x0 h1 y2 h2 y3 h3 x1 h4 y4 h5 y5 x2 h6 y6 h7 y7 x3".split()
 
 
 def tile_attend_gex_w_kernel(tc, xT, dyT, hT, ts, offs, out):
@@ -42,15 +36,22 @@ def tile_attend_gex_w_kernel(tc, xT, dyT, hT, ts, offs, out):
     with ExitStack() as ctx:
         keep = ctx.enter_context(tc.tile_pool(name="keep", bufs=1))
         slots = ctx.enter_context(tc.tile_pool(name="slots", bufs=1))
-        xwork = ctx.enter_context(tc.tile_pool(name="xwork", bufs=2))
+        ring = ctx.enter_context(tc.tile_pool(name="ring", bufs=2))
         turn_psum = ctx.enter_context(tc.psum_pool(name="turn_psum", bufs=1))
         acc_psum = ctx.enter_context(tc.psum_pool(name="acc_psum", bufs=5))
 
-        def tenant(slot, shape, dtype):
-            return slots.tile(shape, dtype, name="tenant", tag=slot, align_bytes=64)
+        made = []
+
+        def tenant(slot, shape, dtype, at=0):
+            made.append(slot)
+            start = WINDOW_BYTES * (LOADS + ["ts_window", "first"]).index(slot) + at
+            return slots.tile(shape, dtype, name="tenant%d" % len(made), align_bytes=64, offset=start)
 
         offsets = keep.tile([P, B * LIST_COLS], U16, name="offsets")
         nc.sync.dma_start(offsets[:], offs)
+
+        def list_of(b):
+            return offsets[:, b * LIST_COLS : (b + 1) * LIST_COLS]
 
         ts_window = tenant("ts_window", [P, T], F32)
         nc.sync.dma_start(ts_window[P - 1 : P, :], ts[0:1, :])
@@ -66,232 +67,175 @@ def tile_attend_gex_w_kernel(tc, xT, dyT, hT, ts, offs, out):
         ident = keep.tile([P, P], F32, name="ident")
         make_identity(nc, ident[:])
 
-        ts_listed = tenant("ts_listed", [P, B * N], F32)
-        nc.vector.tensor_copy(ts_listed[:], ts_window[:].indirect(offsets[:]))
-        ts_cols = [tenant("ts_cols%d" % g, [P, 4], F32) for g in range(B)]
+        ts_listed = keep.tile([P, B * N], F32, name="ts_listed")
+        for b in range(B):
+            nc.vector.tensor_copy(ts_listed[:, b * N : (b + 1) * N], ts_window[:].indirect(list_of(b)))
         ts2 = keep.tile([P, B * N], F32, name="ts2")
-        for g in range(B):
+        ts_cols = [tenant("first", [P, 4], F32, 64 * b) for b in range(B)]
+        for b in range(B):
             bank = acc_psum.tile([P, 4, P], F32, name="acc", tag="acc")
             for c in range(4):
-                s0 = g * N + c * P
+                s0 = b * N + c * P
                 nc.tensor.transpose(bank[:, c, :], ts_listed[:, s0 : s0 + P], ident[:])
-            nc.scalar.copy(ts_cols[g][:], bank[:, :, P - 1])
-        for g in range(B):
+            nc.scalar.copy(ts_cols[b][:], bank[:, :, P - 1])
+        for b in range(B):
             bank = acc_psum.tile([P, 4, P], F32, name="acc", tag="acc")
             for c in range(4):
-                nc.tensor.transpose(bank[:, c, :], ts_cols[g][:, c : c + 1].to_broadcast([P, P]), ident[:])
-            nc.scalar.activation(ts2[:, g * N : (g + 1) * N], bank[:].rearrange("p c s -> p (c s)"), COPY, scale=2.0)
+                nc.tensor.transpose(bank[:, c, :], ts_cols[b][:, c : c + 1].to_broadcast([P, P]), ident[:])
+            nc.scalar.activation(ts2[:, b * N : (b + 1) * N], bank[:].rearrange("p c s -> p (c s)"), COPY, scale=2.0)
 
-        dz_turned = {0: keep.tile([P, B, 4 * BANK], BF16, name="dz_turned", align_bytes=64)}
-        dz_scales = keep.tile([P, B, DV], U8, name="dz_scales", align_bytes=64)
+        landing_tiles = [keep.tile([P, 11 * 2 * P], F32, name="landing%d" % half, align_bytes=64) for half in range(2)]
+        dz_scales = [keep.tile([P, B, BANK], U8, name="dz_scales%d" % half, align_bytes=64) for half in range(2)]
         x_scales = keep.tile([P, D_BLOCKS, B * P], U8, name="x_scales", align_bytes=64)
+        x_turned, x_banks, x_bf16 = {}, {}, {}
+        spare, dy_listed, dz_codes, x_codes = {}, {}, {}, {}
 
-        h_listed, dy_listed, x_turned, x_codes, dz_codes, banks = {}, {}, {}, {}, {}, {}
+        def turn(listed, tag, nb):
+            pairs = listed.bitcast(F32)
+            bank = turn_psum.tile([P, nb, 2, P], F32, name="turn", tag=tag)
+            for b in range(nb):
+                for u in range(2):
+                    nc.tensor.transpose(bank[:, b, u, :], pairs[:, 256 * b + u : 256 * (b + 1) : 2], ident[:])
+            return bank[:].rearrange("p b u r -> p b r u")
 
-        def list_of(b0, nb):
-            return offsets[:, b0 * LIST_COLS : (b0 + nb) * LIST_COLS]
+        def gather_dy(j):
+            nc.vector.tensor_tensor(dy_listed[j], window["y%d" % j][:].indirect(offsets[:]), ts2[:], MULT)
+            if j + 1 < N_BLOCKS:
+                dy_listed[j + 1] = tenant({0: "ts_window", 5: "y3"}.get(j, "y%d" % j), [P, B * N], F32)[:]
 
-        def copy_on(engine, dst, src):
-            if engine == "scalar":
-                nc.scalar.copy(dst, src)
-            else:
-                nc.vector.tensor_copy(dst, src)
+        def landing(j):
+            words = landing_tiles[j // 4][:, 0 : B * 2 * BANK].rearrange("p (b j r u) -> p b j r u", b=B, j=4, u=2)
+            return words[:, :, j % 4]
+
+        h_listed, dz_room = {}, {}
+        dy_listed[0] = keep.tile([P, B * N], F32, name="first_dy")[:]
 
         def gather_h(j):
-            listed = tenant(H_SLOT[j], [P, B * N], F32)
-            nc.vector.tensor_copy(listed[:], window["h%d" % j][:].indirect(offsets[:]))
-            h_listed[j] = tenant(RELU_SLOT[j], [P, B * N], F32) if j in RELU_SLOT and j in ON_GPSIMD else listed
-            if j in ON_GPSIMD:
-                nc.scalar.activation(h_listed[j][:], listed[:], RELU)
+            room = tenant(ROOMS.get(j, "h%d" % (j - 1)), [P, 3 * N], F32) if j else tenant("first", [P, 3 * N], F32)
+            h_listed[j], dz_room[j] = room[:, 0 : B * N], room[:, B * N : 3 * N].bitcast(BF16)
+            raw = h_listed[j] if j else landing_tiles[1][:, 0 : B * N]
+            if 0 < j < N_BLOCKS - 1:
+                start = 2 * BANK + 2 * P * ((j - 1) % 4)
+                raw = landing_tiles[(j - 1) // 4][:, start : start + B * N]
+            nc.vector.tensor_copy(raw, window["h%d" % j][:].indirect(offsets[:]))
+            if j < N_BLOCKS - 1:
+                nc.scalar.activation(h_listed[j], raw, RELU)
 
-        def gather_dy(j, b0, nb):
-            dy_listed[j, b0] = tenant(DY_SLOT[j, b0], [P, nb * N], F32)
-            nc.vector.tensor_tensor(
-                dy_listed[j, b0][:], window["y%d" % j][:].indirect(list_of(b0, nb)), ts2[:, b0 * N : (b0 + nb) * N], MULT
-            )
+        def form_dz(j):
+            dz = dz_room[j] if j else tenant("y1", [P, B * N], BF16, HALF)[:]
+            nc.gpsimd.tensor_tensor(dz, h_listed[j], dy_listed[j], MULT)
+            nc.scalar.copy(landing(j), turn(dz, bank_of[j], B))
 
-        def form_dz(j, b0, nb):
-            dz = tenant(DZ_SLOT.get(j, "dz%d_%d" % (j, b0)), [P, nb * N], BF16)
-            h = h_listed[j][:, b0 * N : (b0 + nb) * N]
-            dy = dy_listed[j, b0][:]
-            if j in ON_GPSIMD:
-                nc.gpsimd.tensor_tensor(dz[:], h, dy, MULT)
-            else:
-                nc.vector.scalar_tensor_tensor(dz[:], h, 0.0, dy, MAX, MULT)
-            pairs = dz[:].bitcast(F32)
-            banks[j, b0] = turn_psum.tile([P, nb, 2, P], F32, name="turn", tag=DZ_BANK[j + b0])
-            for b in range(nb):
-                for u in range(2):
-                    nc.tensor.transpose(banks[j, b0][:, b, u, :], pairs[:, 256 * b + u : 256 * (b + 1) : 2], ident[:])
+        def last_dz(j, b):
+            cols = slice(b * N, (b + 1) * N)
+            nc.vector.tensor_tensor(dy_listed[j][:, cols], window["y%d" % j][:].indirect(list_of(b)), ts2[:, cols], MULT)
+            nc.vector.scalar_tensor_tensor(dz_room[j][:, cols], h_listed[j][:, cols], 0.0, dy_listed[j][:, cols], MAX, MULT)
+            nc.scalar.copy(landing(j)[:, b : b + 1], turn(dz_room[j][:, cols], "BC"[b], 1))
 
-        def land_dz(j, b0, nb, engine):
-            if j == 4:
-                dz_turned[1] = tenant(TURNED_SLOT, [P, B, 4 * BANK], BF16)
-            dst = dz_turned[j // 4][:].bitcast(F32)[:, b0 : b0 + nb, 2 * P * (j % 4) : 2 * P * (j % 4 + 1)]
-            copy_on(engine, dst.rearrange("p b (r u) -> p b r u", u=2), banks[j, b0][:].rearrange("p b u r -> p b r u"))
+        def last_x(i, b):
+            listed = tenant("x1", [P, N], BF16, HALF * b)
+            nc.vector.tensor_copy(listed[:], window["x%d" % i][:].indirect(list_of(b)))
+            x_turned[i, b] = tenant("x1", [P, N], BF16, HALF * b + HALF // 2)
+            dst = x_turned[i, b][:].bitcast(F32).rearrange("p (b r u) -> p b r u", b=1, u=2)
+            nc.scalar.copy(dst, turn(listed[:], "AB"[b], 1))
 
-        carved = {}
+        def quantize_last_x(i, b):
+            codes = keep.tile([P, P], U32, name="last_codes%d" % b, align_bytes=64)
+            nc.vector.quantize_mx(codes[:].bitcast(E4M3), x_scales[:, i, b * P : (b + 1) * P], x_turned[i, b][:])
+            x_codes[i, b] = codes[:]
 
-        def carve(slot, words):
-            if slot not in carved:
-                carved[slot] = [tenant(slot, [P, CODE_WORDS[slot]], U32), 0]
-            start = carved[slot][1]
-            carved[slot][1] = start + words
-            return carved[slot][0][:, start : start + words]
-
-        staged = {}
-
-        def stage(slot, banks_wanted):
-            if slot not in staged:
-                staged[slot] = [tenant(slot, [P, STAGE_BANKS[slot], BANK], F32), 0]
-            start = staged[slot][1]
-            staged[slot][1] = start + banks_wanted
-            return staged[slot][0][:, start : start + banks_wanted, :]
-
-        def codes_for_dz(half, tag):
-            dz_codes[half] = carve(tag, B * BANK)
-
-        def quantize_dz(b, j0, j1):
-            half = j0 // 4
+        def quantize_dz(half, b0, nb, j0, j1):
             nc.vector.quantize_mx(
-                dz_codes[half][:, b * BANK + (j0 - 4 * half) * P : b * BANK + (j1 - 4 * half) * P].bitcast(E5M2),
-                dz_scales[:, b, j0 * P : j1 * P],
-                dz_turned[half][:, b, 4 * (j0 - 4 * half) * P : 4 * (j1 - 4 * half) * P],
+                dz_codes[half][:, b0 : b0 + nb, j0 * P : j1 * P].rearrange("p b n -> p (b n)").bitcast(E5M2),
+                dz_scales[half][:, b0 : b0 + nb, j0 * P : j1 * P].rearrange("p b n -> p (b n)"),
+                landing_tiles[half][:, (b0 * 4 + j0) * 2 * P : ((b0 + nb - 1) * 4 + j1) * 2 * P].bitcast(BF16),
             )
 
-        def paired(listed):
-            return listed.rearrange("p (u s e) -> p s u e", u=2, e=2)
+        def cast_x(i):
+            x_bf16[i] = tenant("ts_window", [P, T], BF16, HALF)
+            for c in range(2):
+                cols = slice(c * T // 2, (c + 1) * T // 2)
+                nc.scalar.activation(x_bf16[i][:, cols], window["x%d" % i][:, cols], COPY)
 
-        def turn_x(i, b0, nb, listed, engine):
-            pairs = listed.bitcast(F32)
-            bank = turn_psum.tile([P, nb, 2, P], F32, name="turn", tag=X_BANK[i + b0])
-            for b in range(nb):
-                for u in range(2):
-                    w0 = (u * nb + b) * P
-                    nc.tensor.transpose(bank[:, b, u, :], pairs[:, w0 : w0 + P], ident[:])
-            x_turned[i, b0] = tenant("x_turned%d" % i, [P, nb * 4 * P], BF16)
-            dst = x_turned[i, b0][:].bitcast(F32).rearrange("p (b r u) -> p b r u", b=nb, u=2)
-            copy_on(engine, dst, bank[:].rearrange("p b u r -> p b r u"))
+        def list_x(i, slot, at):
+            listed = tenant(slot, [P, B * N], BF16, at)
+            for b in range(B):
+                nc.scalar.activation(listed[:, b * N : (b + 1) * N], x_bf16[i][:].indirect(list_of(b)), COPY)
+            x_banks[i] = turn(listed[:], "C", B)
 
-        def x_by_scalar(i, tag, engine):
-            x_bf16 = tenant(tag, [P, T], BF16)
-            nc.scalar.activation(x_bf16[:], window["x%d" % i][:], COPY)
-            listed = xwork.tile([P, B * N], BF16, name="x_listed", tag="x_listed")
-            nc.scalar.activation(paired(listed[:]), x_bf16[:].indirect(offsets[:]), COPY)
-            turn_x(i, 0, B, listed[:], engine)
+        def land_x(i, slot):
+            x_turned[i] = tenant(slot, [P, B * 4 * P], BF16, 3 * HALF // 2)
+            dst = x_turned[i][:].bitcast(F32).rearrange("p (b r u) -> p b r u", b=B, u=2)
+            nc.scalar.copy(dst, x_banks[i])
 
-        def gather_x(i, b):
-            nc.vector.tensor_copy(paired(last_listed[:, b, :]), window["x%d" % i][:].indirect(list_of(b, 1)))
-
-        def codes_for_x(i, tag):
-            x_codes[i] = carve(tag, B * P)
-
-        def quantize_x(i, b0, nb):
-            cols = slice(b0 * P, (b0 + nb) * P)
-            nc.vector.quantize_mx(x_codes[i][:, cols].bitcast(E4M3), x_scales[:, i, cols], x_turned[i, b0][:])
+        def quantize_x(i, slot, at=3 * HALF // 2):
+            codes = tenant(slot, [P, B * P], U32, at)
+            nc.vector.quantize_mx(codes[:].bitcast(E4M3), x_scales[:, i, :], x_turned[i][:])
+            for b in range(B):
+                x_codes[i, b] = codes[:, b * P : (b + 1) * P]
 
         def multiply(half, b, i, engine, dst):
             acc = acc_psum.tile([P, BANK], F32, name="acc", tag="acc")
-            d_cols = slice(b * P, (b + 1) * P)
             nc.tensor.matmul_mx(
                 acc[:],
-                lhsT=x_codes[i][:, d_cols].bitcast(E4M3),
-                lhsT_scale=x_scales[:, i, d_cols],
-                rhs=dz_codes[half][:, b * BANK : (b + 1) * BANK].bitcast(E5M2),
-                rhs_scale=dz_scales[:, b, half * BANK : (half + 1) * BANK],
+                lhsT=x_codes[i, b].bitcast(E4M3),
+                lhsT_scale=x_scales[:, i, b * P : (b + 1) * P],
+                rhs=dz_codes[half][:, b, :].bitcast(E5M2),
+                rhs_scale=dz_scales[half][:, b, :],
                 start=True,
                 stop=True,
             )
-            copy_on(engine, dst, acc[:])
+            if engine == "s":
+                nc.scalar.copy(dst, acc[:])
+            else:
+                nc.vector.tensor_copy(dst, acc[:])
 
-        def halves(half, b, i0, i1, slot, engines):
-            result = stage(slot, i1 - i0)
-            for i in range(i0, i1):
-                multiply(half, b, i, engines[i - i0], result[:, i - i0, :])
-            dst = out[b, i0 * P : i1 * P, half * BANK : (half + 1) * BANK]
-            nc.sync.dma_start(dst.rearrange("(i p) n -> p i n", p=P), result)
+        def results(slot, jobs, at=0):
+            staged = tenant(slot, [P, len(jobs), BANK], F32, at)
+            for k, (half, b, i, engine) in enumerate(jobs):
+                multiply(half, b, i, engine, staged[:, k, :])
+                nc.sync.dma_start(out[b, i * P : (i + 1) * P, half * BANK : (half + 1) * BANK], staged[:, k, :])
 
-        def first_half(i, slot, engines):
-            result = stage(slot, B)
-            for b in range(B):
-                multiply(0, b, i, engines[b], result[:, b, :])
-            nc.sync.dma_start(out[:, i * P : (i + 1) * P, 0:BANK].rearrange("b p n -> p b n"), result)
-
-        def last_block(b, i, slot, engines):
-            result = stage(slot, 2)
-            for half in range(2):
-                multiply(half, b, i, engines[half], result[:, half, :])
-            nc.sync.dma_start(out[b, i * P : (i + 1) * P, :], result.rearrange("p h n -> p (h n)"))
-
-        last_listed = None
-        gather_h(0)
-        gather_h(1)
-        gather_dy(0, 0, B)
-        form_dz(0, 0, B)
-        land_dz(0, 0, B, "scalar")
-        gather_h(2)
-        gather_dy(1, 0, B)
-        form_dz(1, 0, B)
-        land_dz(1, 0, B, "scalar")
-        gather_h(3)
-        x_by_scalar(0, "xb", "scalar")
-        gather_dy(2, 0, B)
-        form_dz(2, 0, B)
-        land_dz(2, 0, B, "scalar")
-        gather_h(4)
-        gather_dy(3, 0, B)
-        form_dz(3, 0, B)
-        land_dz(3, 0, B, "scalar")
-        gather_dy(4, 0, B)
-        form_dz(4, 0, B)
-        land_dz(4, 0, B, "scalar")
-        gather_h(5)
-        x_by_scalar(1, "xb", "vector")
-        codes_for_x(1, "h5")
-        quantize_x(1, 0, B)
-        gather_dy(5, 0, B)
-        form_dz(5, 0, B)
-        land_dz(5, 0, B, "scalar")
-        gather_h(6)
-        codes_for_dz(0, "h6")
-        quantize_dz(0, 0, 4)
-        quantize_dz(1, 0, 4)
-        first_half(1, "first0", ["scalar", "scalar"])
-        gather_dy(6, 0, B)
-        form_dz(6, 0, B)
-        land_dz(6, 0, B, "scalar")
-        x_by_scalar(2, "xb", "scalar")
-        codes_for_x(2, "h4")
-        quantize_x(2, 0, B)
-        halves(0, 0, 2, 3, "first1", ["scalar"])
-        halves(0, 1, 2, 3, "first1", ["scalar"])
-        gather_h(7)
-        gather_dy(7, 0, 1)
-        form_dz(7, 0, 1)
-        gather_dy(7, 1, 1)
-        land_dz(7, 0, 1, "vector")
-        form_dz(7, 1, 1)
-        codes_for_x(0, "y7")
-        quantize_x(0, 0, B)
-        halves(0, 0, 0, 1, "ts_cols0", ["scalar"])
-        halves(0, 1, 0, 1, "ts_cols0", ["scalar"])
-        codes_for_dz(1, "c1")
-        quantize_dz(0, 4, 8)
-        land_dz(7, 1, 1, "vector")
-        quantize_dz(1, 4, 8)
-        halves(1, 0, 0, 1, "ts_cols1", ["scalar"])
-        halves(1, 0, 1, 2, "ts_cols1", ["scalar"])
-        halves(1, 0, 2, 3, "h3", ["scalar"])
-        halves(1, 1, 0, 1, "h3", ["scalar"])
-        halves(1, 1, 1, 2, "h3", ["scalar"])
-        halves(1, 1, 2, 3, "h3", ["scalar"])
-        last_listed = tenant("xl", [P, B, N], BF16)
-        gather_x(3, 0)
-        gather_x(3, 1)
-        codes_for_x(3, "c3")
-        turn_x(3, 0, 1, last_listed[:, 0, :], "vector")
-        quantize_x(3, 0, 1)
-        turn_x(3, 1, 1, last_listed[:, 1, :], "vector")
-        quantize_x(3, 1, 1)
-        last_block(0, 3, "y3", ["scalar", "vector"])
-        last_block(1, 3, "y3", ["scalar", "vector"])
+        bank_of = "ABABABA"
+        for key in LOADS[:-2]:
+            j = int(key[1])
+            if key[0] == "h":
+                gather_h(j)
+            elif key[0] == "y":
+                gather_dy(j)
+            else:
+                cast_x(j)
+            if key == "x0":
+                list_x(0, "x0", 0)
+            if key == "y5":
+                quantize_x(1, "y5", HALF // 2)
+                dz_codes[0] = tenant("y5", [P, B, BANK], U32, HALF)
+                quantize_dz(0, 0, B, 0, 4)
+                dz_room[5] = landing_tiles[0][:, 0:N].bitcast(BF16)
+            if key in X_LANDS:
+                land_x(X_LANDS[key], key)
+            if key == "h3":
+                quantize_x(0, "h3", HALF)
+            if key[0] == "h" and j:
+                form_dz(j - 1)
+            if key == "h4":
+                list_x(1, "h4", 3 * HALF // 2)
+            if key == "x2":
+                results("x2", [(0, b, 0, "s") for b in range(B)])
+            if key == "h6":
+                list_x(2, "h6", 3 * HALF // 2)
+                results("ts_window", [(0, b, 1, "s") for b in range(B)], HALF)
+        dz_codes[1] = tenant("x0", [P, B, BANK], U32, HALF)
+        for b in range(B):
+            last_dz(N_BLOCKS - 1, b)
+        quantize_x(2, "y7")
+        results("h0", [(0, b, 2, "s") for b in range(B)])
+        quantize_dz(1, 0, 1, 0, 4)
+        results("y0", [(1, 0, i, "s") for i in range(3)])
+        last_x(3, 0)
+        quantize_dz(1, 1, 1, 0, 4)
+        results("y1", [(1, 1, i, "s") for i in range(3)])
+        quantize_last_x(3, 0)
+        last_x(3, 1)
+        quantize_last_x(3, 1)
+        results("y2", [(half, b, 3, "sv"[half]) for b in range(B) for half in range(2)])

@@ -135,9 +135,12 @@ def tile_attend_gex_w_kernel(tc, xT, dyT, hT, ts, offs, out):
         def last_x(i, b):
             listed = tenant("x1", [P, N], BF16, HALF * b)
             nc.vector.tensor_copy(listed[:], window["x%d" % i][:].indirect(list_of(b)))
+            x_banks[i, b] = turn(listed[:], "AB"[b], 1)
+
+        def land_last_x(i, b):
             x_turned[i, b] = tenant("x1", [P, N], BF16, HALF * b + HALF // 2)
             dst = x_turned[i, b][:].bitcast(F32).rearrange("p (b r u) -> p b r u", b=1, u=2)
-            nc.scalar.copy(dst, turn(listed[:], "AB"[b], 1))
+            nc.vector.tensor_copy(dst, x_banks[i, b])
 
         def quantize_last_x(i, b):
             codes = keep.tile([P, P], U32, name="last_codes%d" % b, align_bytes=64)
@@ -235,7 +238,8 @@ def tile_attend_gex_w_kernel(tc, xT, dyT, hT, ts, offs, out):
         last_x(3, 0)
         quantize_dz(1, 1, 1, 0, 4)
         results("y1", [(1, 1, i, "s") for i in range(3)])
-        quantize_last_x(3, 0)
         last_x(3, 1)
-        quantize_last_x(3, 1)
-        results("y2", [(half, b, 3, "sv"[half]) for b in range(B) for half in range(2)])
+        for b in range(B):
+            land_last_x(3, b)
+            quantize_last_x(3, b)
+        results("y2", [(half, b, 3, "vs"[half]) for b in range(B) for half in range(2)])

@@ -242,4 +242,8 @@ def tile_attend_gex_w_kernel(tc, xT, dyT, hT, ts, offs, out):
         for b in range(B):
             land_last_x(3, b)
             quantize_last_x(3, b)
-        results("y2", [(half, b, 3, "vs"[half]) for b in range(B) for half in range(2)])
+        for b in range(B):
+            rows = tenant("y2", [P, DV], F32, HALF * b)
+            for half in range(2):
+                multiply(half, b, 3, "vs"[half], rows[:, half * BANK : (half + 1) * BANK])
+            nc.sync.dma_start(out[b, 3 * P : 4 * P, :], rows[:])

from contextlib import ExitStack

import concourse.mybir as mybir
from concourse.masks import make_identity

B, N, T, D, DV = 2, 512, 2048, 512, 1024
FLOPS = 2 * B * N * D * DV
BYTES = 4 * (D * T + 2 * DV * T + T + B * D * DV) + 2 * 128 * B * N // 16

F32 = mybir.dt.float32
BF16 = mybir.dt.bfloat16
U32 = mybir.dt.uint32
U16 = mybir.dt.uint16
U8 = mybir.dt.uint8
E4M3 = mybir.dt.float8_e4m3fn_x4
E5M2 = mybir.dt.float8_e5m2_x4
MULT = mybir.AluOpType.mult
MAX = mybir.AluOpType.max
COPY = mybir.ActivationFunctionType.Copy
RELU = mybir.ActivationFunctionType.Relu

P = 128
BANK = 512
LIST_COLS = N // 16
D_BLOCKS = D // P
N_BLOCKS = DV // P
WINDOW_BYTES = 4 * T
X_LANDS = {"h1": 0, "h5": 1, "h7": 2}
ROOMS = {4: "h0"}
HALF = WINDOW_BYTES // 2
LOADS = "h0 y0 y1 x0 h1 y2 h2 y3 h3 x1 h4 y4 h5 y5 x2 h6 y6 h7 y7 x3".split()


def tile_attend_gex_w_kernel(tc, xT, dyT, hT, ts, offs, out):
    nc = tc.nc
    with ExitStack() as ctx:
        keep = ctx.enter_context(tc.tile_pool(name="keep", bufs=1))
        slots = ctx.enter_context(tc.tile_pool(name="slots", bufs=1))
        ring = ctx.enter_context(tc.tile_pool(name="ring", bufs=2))
        turn_psum = ctx.enter_context(tc.psum_pool(name="turn_psum", bufs=1))
        acc_psum = ctx.enter_context(tc.psum_pool(name="acc_psum", bufs=5))

        made = []

        def tenant(slot, shape, dtype, at=0):
            made.append(slot)
            start = WINDOW_BYTES * (LOADS + ["ts_window", "first"]).index(slot) + at
            return slots.tile(shape, dtype, name="tenant%d" % len(made), align_bytes=64, offset=start)

        offsets = keep.tile([P, B * LIST_COLS], U16, name="offsets")
        nc.sync.dma_start(offsets[:], offs)

        def list_of(b):
            return offsets[:, b * LIST_COLS : (b + 1) * LIST_COLS]

        ts_window = tenant("ts_window", [P, T], F32)
        nc.sync.dma_start(ts_window[P - 1 : P, :], ts[0:1, :])
        nc.vector.memset(ts_window[0 : P - 1, :], 0.0)

        sources = {"h": hT, "y": dyT, "x": xT}
        window = {}
        for key in LOADS:
            j = int(key[1])
            window[key] = tenant(key, [P, T], F32)
            nc.sync.dma_start(window[key][:], sources[key[0]][j * P : (j + 1) * P, :])

        ident = keep.tile([P, P], F32, name="ident")
        make_identity(nc, ident[:])

        ts_listed = keep.tile([P, B * N], F32, name="ts_listed")
        for b in range(B):
            nc.vector.tensor_copy(ts_listed[:, b * N : (b + 1) * N], ts_window[:].indirect(list_of(b)))
        ts2 = keep.tile([P, B * N], F32, name="ts2")
        ts_cols = [tenant("first", [P, 4], F32, 64 * b) for b in range(B)]
        for b in range(B):
            bank = acc_psum.tile([P, 4, P], F32, name="acc", tag="acc")
            for c in range(4):
                s0 = b * N + c * P
                nc.tensor.transpose(bank[:, c, :], ts_listed[:, s0 : s0 + P], ident[:])
            nc.scalar.copy(ts_cols[b][:], bank[:, :, P - 1])
        for b in range(B):
            bank = acc_psum.tile([P, 4, P], F32, name="acc", tag="acc")
            for c in range(4):
                nc.tensor.transpose(bank[:, c, :], ts_cols[b][:, c : c + 1].to_broadcast([P, P]), ident[:])
            nc.scalar.activation(ts2[:, b * N : (b + 1) * N], bank[:].rearrange("p c s -> p (c s)"), COPY, scale=2.0)

        landing_tiles = [keep.tile([P, 11 * 2 * P], F32, name="landing%d" % half, align_bytes=64) for half in range(2)]
        dz_scales = [keep.tile([P, B, BANK], U8, name="dz_scales%d" % half, align_bytes=64) for half in range(2)]
        x_scales = keep.tile([P, D_BLOCKS, B * P], U8, name="x_scales", align_bytes=64)
        x_turned, x_banks, x_bf16 = {}, {}, {}
        spare, dy_listed, dz_codes, x_codes = {}, {}, {}, {}

        def turn(listed, tag, nb):
            pairs = listed.bitcast(F32)
            bank = turn_psum.tile([P, nb, 2, P], F32, name="turn", tag=tag)
            for b in range(nb):
                for u in range(2):
                    nc.tensor.transpose(bank[:, b, u, :], pairs[:, 256 * b + u : 256 * (b + 1) : 2], ident[:])
            return bank[:].rearrange("p b u r -> p b r u")

        def gather_dy(j):
            nc.vector.tensor_tensor(dy_listed[j], window["y%d" % j][:].indirect(offsets[:]), ts2[:], MULT)
            if j + 1 < N_BLOCKS:
                dy_listed[j + 1] = tenant({0: "ts_window", 5: "y3"}.get(j, "y%d" % j), [P, B * N], F32)[:]

        def landing(j):
            words = landing_tiles[j // 4][:, 0 : B * 2 * BANK].rearrange("p (b j r u) -> p b j r u", b=B, j=4, u=2)
            return words[:, :, j % 4]

        h_listed, dz_room = {}, {}
        dy_listed[0] = keep.tile([P, B * N], F32, name="first_dy")[:]

        def gather_h(j):
            room = tenant(ROOMS.get(j, "h%d" % (j - 1)), [P, 3 * N], F32) if j else tenant("first", [P, 3 * N], F32)
            h_listed[j], dz_room[j] = room[:, 0 : B * N], room[:, B * N : 3 * N].bitcast(BF16)
            raw = h_listed[j] if j else landing_tiles[1][:, 0 : B * N]
            if 0 < j < N_BLOCKS - 1:
                start = 2 * BANK + 2 * P * ((j - 1) % 4)
                raw = landing_tiles[(j - 1) // 4][:, start : start + B * N]
            nc.vector.tensor_copy(raw, window["h%d" % j][:].indirect(offsets[:]))
            if j < N_BLOCKS - 1:
                nc.scalar.activation(h_listed[j], raw, RELU)

        def form_dz(j):
            dz = dz_room[j] if j else tenant("y1", [P, B * N], BF16, HALF)[:]
            nc.gpsimd.tensor_tensor(dz, h_listed[j], dy_listed[j], MULT)
            nc.scalar.copy(landing(j), turn(dz, bank_of[j], B))

        def last_dz(j, b):
            cols = slice(b * N, (b + 1) * N)
            nc.vector.tensor_tensor(dy_listed[j][:, cols], window["y%d" % j][:].indirect(list_of(b)), ts2[:, cols], MULT)
            nc.vector.scalar_tensor_tensor(dz_room[j][:, cols], h_listed[j][:, cols], 0.0, dy_listed[j][:, cols], MAX, MULT)
            nc.scalar.copy(landing(j)[:, b : b + 1], turn(dz_room[j][:, cols], "BC"[b], 1))

        def last_x(i, b):
            listed = tenant("x1", [P, N], BF16, HALF * b)
            nc.vector.tensor_copy(listed[:], window["x%d" % i][:].indirect(list_of(b)))
            x_banks[i, b] = turn(listed[:], "AB"[b], 1)

        def land_last_x(i, b):
            x_turned[i, b] = tenant("x1", [P, N], BF16, HALF * b + HALF // 2)
            dst = x_turned[i, b][:].bitcast(F32).rearrange("p (b r u) -> p b r u", b=1, u=2)
            nc.vector.tensor_copy(dst, x_banks[i, b])

        def quantize_last_x(i, b):
            codes = keep.tile([P, P], U32, name="last_codes%d" % b, align_bytes=64)
            nc.vector.quantize_mx(codes[:].bitcast(E4M3), x_scales[:, i, b * P : (b + 1) * P], x_turned[i, b][:])
            x_codes[i, b] = codes[:]

        def quantize_dz(half, b0, nb, j0, j1):
            nc.vector.quantize_mx(
                dz_codes[half][:, b0 : b0 + nb, j0 * P : j1 * P].rearrange("p b n -> p (b n)").bitcast(E5M2),
                dz_scales[half][:, b0 : b0 + nb, j0 * P : j1 * P].rearrange("p b n -> p (b n)"),
                landing_tiles[half][:, (b0 * 4 + j0) * 2 * P : ((b0 + nb - 1) * 4 + j1) * 2 * P].bitcast(BF16),
            )

        def cast_x(i):
            x_bf16[i] = tenant("ts_window", [P, T], BF16, HALF)
            for c in range(2):
                cols = slice(c * T // 2, (c + 1) * T // 2)
                nc.scalar.activation(x_bf16[i][:, cols], window["x%d" % i][:, cols], COPY)

        def list_x(i, slot, at):
            listed = tenant(slot, [P, B * N], BF16, at)
            for b in range(B):
                nc.scalar.activation(listed[:, b * N : (b + 1) * N], x_bf16[i][:].indirect(list_of(b)), COPY)
            x_banks[i] = turn(listed[:], "C", B)

        def land_x(i, slot):
            x_turned[i] = tenant(slot, [P, B * 4 * P], BF16, 3 * HALF // 2)
            dst = x_turned[i][:].bitcast(F32).rearrange("p (b r u) -> p b r u", b=B, u=2)
            nc.scalar.copy(dst, x_banks[i])

        def quantize_x(i, slot, at=3 * HALF // 2):
            codes = tenant(slot, [P, B * P], U32, at)
            nc.vector.quantize_mx(codes[:].bitcast(E4M3), x_scales[:, i, :], x_turned[i][:])
            for b in range(B):
                x_codes[i, b] = codes[:, b * P : (b + 1) * P]

        def multiply(half, b, i, engine, dst):
            acc = acc_psum.tile([P, BANK], F32, name="acc", tag="acc")
            nc.tensor.matmul_mx(
                acc[:],
                lhsT=x_codes[i, b].bitcast(E4M3),
                lhsT_scale=x_scales[:, i, b * P : (b + 1) * P],
                rhs=dz_codes[half][:, b, :].bitcast(E5M2),
                rhs_scale=dz_scales[half][:, b, :],
                start=True,
                stop=True,
            )
            if engine == "s":
                nc.scalar.copy(dst, acc[:])
            else:
                nc.vector.tensor_copy(dst, acc[:])

        def results(slot, jobs, at=0):
            staged = tenant(slot, [P, len(jobs), BANK], F32, at)
            for k, (half, b, i, engine) in enumerate(jobs):
                multiply(half, b, i, engine, staged[:, k, :])
                nc.sync.dma_start(out[b, i * P : (i + 1) * P, half * BANK : (half + 1) * BANK], staged[:, k, :])

        bank_of = "ABABABA"
        for key in LOADS[:-2]:
            j = int(key[1])
            if key[0] == "h":
                gather_h(j)
            elif key[0] == "y":
                gather_dy(j)
            else:
                cast_x(j)
            if key == "x0":
                list_x(0, "x0", 0)
            if key == "y5":
                quantize_x(1, "y5", HALF // 2)
                dz_codes[0] = tenant("y5", [P, B, BANK], U32, HALF)
                quantize_dz(0, 0, B, 0, 4)
                dz_room[5] = landing_tiles[0][:, 0:N].bitcast(BF16)
            if key in X_LANDS:
                land_x(X_LANDS[key], key)
            if key == "h3":
                quantize_x(0, "h3", HALF)
            if key[0] == "h" and j:
                form_dz(j - 1)
            if key == "h4":
                list_x(1, "h4", 3 * HALF // 2)
            if key == "x2":
                results("x2", [(0, b, 0, "s") for b in range(B)])
            if key == "h6":
                list_x(2, "h6", 3 * HALF // 2)
                results("ts_window", [(0, b, 1, "s") for b in range(B)], HALF)
        dz_codes[1] = tenant("x0", [P, B, BANK], U32, HALF)
        for b in range(B):
            last_dz(N_BLOCKS - 1, b)
        quantize_x(2, "y7")
        results("h0", [(0, b, 2, "s") for b in range(B)])
        quantize_dz(1, 0, 1, 0, 4)
        results("y0", [(1, 0, i, "s") for i in range(3)])
        last_x(3, 0)
        quantize_dz(1, 1, 1, 0, 4)
        results("y1", [(1, 1, i, "s") for i in range(3)])
        last_x(3, 1)
        for b in range(B):
            land_last_x(3, b)
            quantize_last_x(3, b)
        for b in range(B):
            rows = tenant("y2", [P, DV], F32, HALF * b)
            for half in range(2):
                multiply(half, b, 3, "vs"[half], rows[:, half * BANK : (half + 1) * BANK])
            nc.sync.dma_start(out[b, 3 * P : 4 * P, :], rows[:])
